import numpy as np
import ml_dtypes


def mxq(x, axis, fmt="e4m3"):
    dtype, down = {"e4m3": (ml_dtypes.float8_e4m3fn, 7), "e5m2": (ml_dtypes.float8_e5m2, 14)}[fmt]
    v = np.moveaxis(np.asarray(x, np.float32).astype(ml_dtypes.bfloat16).astype(np.float64), axis, -1)
    blocks = v.reshape(v.shape[:-1] + (-1, 32))
    amax = np.abs(blocks).max(-1, keepdims=True)
    byte = np.maximum(np.where(amax > 0, np.frexp(amax)[1] - 1 + 127, 0) - down, 1)
    scale = np.exp2(byte - 127.0)
    codes = (blocks / scale).astype(np.float32).astype(dtype).astype(np.float64)
    return np.moveaxis((codes * scale).reshape(v.shape), -1, axis)


WIDE = False


def mx_kscale(k):
    if not WIDE:
        return np.ones(k)
    levels = np.array([10, -10, 5, -5, 0])
    if k % 512:
        return np.exp2(np.random.permutation(np.resize(levels, k // 32))).repeat(32)
    a = np.empty((k // 512, 16))
    for p in range(k // 512):
        a[p, :8] = np.random.permutation(np.resize(levels, 8))
        for g in range(8):
            far = levels[np.abs(levels - a[p, g]) >= 10]
            a[p, g + 8] = far[np.random.randint(len(far))]
    return np.exp2(a.ravel()).repeat(32)


def f64(x):
    return np.asarray(x).astype(np.float64)


def striped(idx):
    return np.tile(idx.reshape(-1, 16).T, (8, 1)).astype(np.uint16)


def unstriped(offs):
    return offs[:16].T.reshape(-1).astype(np.int64)


def pack_weight(w):
    k, n = w.shape
    w = f64(np.asarray(w, np.float32).astype(ml_dtypes.bfloat16)).reshape(k // 32, 32, n)
    amax = np.abs(w).max(1)
    byte = np.clip(np.where(amax > 0, np.frexp(amax)[1] - 1 + 127 - 7, 1), 1, 254)
    scaled = (w * np.exp2(127.0 - byte)[:, None, :]).reshape(k, n).astype(np.float32)
    words = np.ascontiguousarray(scaled.reshape(k // 512, 128, 4, n).transpose(0, 1, 3, 2)).astype(ml_dtypes.float8_e4m3fn).view(np.uint8)
    return words, np.ascontiguousarray(byte.astype(np.uint8).reshape(k // 512, 16, n))


def unpack_weight(words, scales):
    g, p, n, _ = words.shape
    vals = np.ascontiguousarray(words).view(ml_dtypes.float8_e4m3fn).astype(np.float64) * np.repeat(np.exp2(scales.astype(np.float64) - 127.0), 8, axis=1)[..., None]
    return vals.transpose(0, 1, 3, 2).reshape(g * 512, n)


E2M1 = np.array([0.0, 0.5, 1.0, 1.5, 2.0, 3.0, 4.0, 6.0, -0.0, -0.5, -1.0, -1.5, -2.0, -3.0, -4.0, -6.0])


def pack_fp4(w):
    k, n = w.shape
    w = f64(np.asarray(w, np.float32).astype(ml_dtypes.bfloat16)).reshape(k // 32, 32, n)
    amax = np.abs(w).max(1)
    mant, ex = np.frexp(amax / 6.0)
    byte = np.clip(np.where(amax > 0, np.where(mant > 0.5, ex, ex - 1) + 127, 1), 1, 254)
    scaled = (w * np.exp2(127.0 - byte)[:, None, :]).reshape(k, n).astype(np.float32)
    c = np.ascontiguousarray(scaled.reshape(k // 512, 128, 4, n).transpose(0, 1, 3, 2)).astype(ml_dtypes.float4_e2m1fn).view(np.uint8) & 0xF
    words = (c[..., 0::2] | (c[..., 1::2] << 4)).reshape(k // 512, 128, 2 * n)
    return np.ascontiguousarray(words), np.ascontiguousarray(byte.astype(np.uint8).reshape(k // 512, 16, n))


def unpack_fp4(words, scales):
    g, _, n = scales.shape
    words = np.ascontiguousarray(words).reshape(g, 128, n, 2)
    nib = np.empty((g, 128, n, 4), np.uint8)
    nib[..., 0::2] = words & 0xF
    nib[..., 1::2] = words >> 4
    vals = E2M1[nib] * np.repeat(np.exp2(scales.astype(np.float64) - 127.0), 8, axis=1)[..., None]
    return vals.transpose(0, 1, 3, 2).reshape(g * 512, n)


def sigmoid(v):
    return 1.0 / (1.0 + np.exp(-np.maximum(v, -700.0)))


K, T, S, N, H = 512, 2048, 512, 256, 512


def setup_inputs():
    n = np.random.standard_normal
    s = mx_kscale(K)[:, None]
    u = mx_kscale(H)
    packed_xT = pack_weight(n((K, T)) * s)
    packed_w1 = pack_fp4(n((K, H)) / np.sqrt(K) / s)
    packed_w2 = pack_fp4(n((K, H)) / np.sqrt(K) / s)
    packed_w3 = pack_fp4(n((H, N)) / np.sqrt(H) / u[:, None])
    return {
        "x_words": packed_xT[0],
        "x_scales": packed_xT[1],
        "w1_words": packed_w1[0],
        "w1_scales": packed_w1[1],
        "w2_words": packed_w2[0],
        "w2_scales": packed_w2[1],
        "unit": (np.random.uniform(0.6, 1.4, (H, 1)) * u[:, None]).astype(np.float32),
        "w3_words": packed_w3[0],
        "w3_scales": packed_w3[1],
        "offs": striped(np.random.permutation(T)[:S]),
        "e1": striped(np.random.permutation(S)),
        "e2": striped(np.random.permutation(S)),
        "fc": striped(np.random.permutation(S)),
    }


def reference(x_words, x_scales, w1_words, w1_scales, w2_words, w2_scales, unit, w3_words, w3_scales, offs, e1, e2, fc):
    xq = unpack_weight(x_words, x_scales)[:, unstriped(offs)]
    ft = unpack_fp4(w1_words, w1_scales).T @ xq
    fa = ft[:, unstriped(e1)]
    sd = unpack_fp4(w2_words, w2_scales).T @ xq
    sa = sd[:, unstriped(e1)]
    s1 = np.tanh(sa)
    sb = sd[:, unstriped(e2)]
    s2 = np.tanh(sb)
    tt = (np.abs(s1) + 0.1) / (np.abs(s1) + np.abs(s2) + 0.2)
    fb = ft[:, unstriped(e2)]
    vert = fa * (-1.0 * tt + 1.0) + fb * tt
    cross = sigmoid(-4.0 * (s1 * s2))
    cs = cross * s1
    vf = vert[:, unstriped(fc)] - cs[:, unstriped(fc)]
    hid = f64(unit) * vf
    return unpack_fp4(w3_words, w3_scales).T @ mxq(hid, 0, "e4m3")

@@ -1,0 +1,277 @@
+from contextlib import ExitStack
+
+import concourse.mybir as mybir
+from concourse.masks import make_identity
+
+K, T, S, N, H = 512, 2048, 512, 256, 512
+FLOPS = 2 * K * H * S * 2 + 2 * H * N * S
+
+F32 = mybir.dt.float32
+BF16 = mybir.dt.bfloat16
+I32 = mybir.dt.int32
+U32 = mybir.dt.uint32
+U16 = mybir.dt.uint16
+U8 = mybir.dt.uint8
+FP8X4 = mybir.dt.float8_e4m3fn_x4
+FP4X4 = mybir.dt.float4_e2m1fn_x4
+ACT = mybir.ActivationFunctionType
+ALU = mybir.AluOpType
+
+P = 128
+TILES = H // P
+BLOCKS = S // P
+HALF = S // 2
+LIST_COLS = S // 16
+SCALAR_FEATURE_TILES = 2
+
+
+def tile_picked_ymarch_off_p_kernel(
+    tc, x_words, x_scales, w1_words, w1_scales, w2_words, w2_scales, unit, w3_words, w3_scales, offs, e1, e2, fc, out
+):
+    nc = tc.nc
+    with ExitStack() as ctx:
+        keep = ctx.enter_context(tc.tile_pool(name="keep", bufs=1))
+        psum = ctx.enter_context(tc.psum_pool(name="psum", bufs=1))
+
+        def sb(name, width, dtype=F32):
+            return keep.tile([P, width], dtype, name=name, align_bytes=64)
+
+        def bank(slot, name):
+            return psum.tile([P, S], F32, name=name, tag="bank%d" % slot)
+
+        def cols(i, width):
+            return slice(i * width, (i + 1) * width)
+
+        def half_of(lst, h):
+            return lst[:, cols(h, LIST_COLS // 2)]
+
+        def load_scales(queue, tile_cols, src):
+            for q in range(4):
+                queue.dma_start(out=tile_cols[32 * q : 32 * q + 4, :].bitcast(I32), in_=src[0, 4 * q : 4 * q + 4, :].bitcast(I32))
+
+        offs_sb = keep.tile([P, LIST_COLS], U16, name="offs_sb")
+        e1_sb = keep.tile([P, LIST_COLS], U16, name="e1_sb")
+        e2_sb = keep.tile([P, LIST_COLS], U16, name="e2_sb")
+        fc_sb = keep.tile([P, LIST_COLS], U16, name="fc_sb")
+        xw = sb("xw", T, U32)
+        xs = sb("xs", T, U8)
+        w1w = sb("w1w", 2 * H, U8)
+        w2w = sb("w2w", 2 * H, U8)
+        w3w = sb("w3w", 2 * N, U8)
+        w1s = sb("w1s", H, U8)
+        w2s = sb("w2s", H, U8)
+        w3s = sb("w3s", N, U8)
+        unit_sb = sb("unit_sb", TILES)
+        ident = sb("ident", P)
+
+        nc.vector.memset(xs[:].bitcast(I32), 0)
+        nc.vector.memset(w2s[:].bitcast(I32), 0)
+        nc.vector.memset(w1s[:].bitcast(I32), 0)
+        nc.vector.memset(w3s[:].bitcast(I32), 0)
+        nc.gpsimd.dma_start(out=w2w[:].bitcast(I32), in_=w2_words[0].bitcast(I32))
+        nc.sync.dma_start(out=offs_sb[:], in_=offs)
+        nc.sync.dma_start(out=xw[:].bitcast(I32), in_=x_words[0].rearrange("p n t -> p (n t)").bitcast(I32))
+        load_scales(nc.scalar, xs, x_scales)
+        load_scales(nc.scalar, w2s, w2_scales)
+        nc.sync.dma_start(out=e1_sb[:], in_=e1)
+        nc.sync.dma_start(out=e2_sb[:], in_=e2)
+        nc.sync.dma_start(out=fc_sb[:], in_=fc)
+        nc.gpsimd.dma_start(out=w1w[:].bitcast(I32), in_=w1_words[0].bitcast(I32))
+        load_scales(nc.sync, w1s, w1_scales)
+        with nc.allow_non_contiguous_dma(reason="one value a partition"):
+            nc.gpsimd.dma_start(out=unit_sb[:].rearrange("p (t o) -> p t o", o=1), in_=unit.rearrange("(t p) o -> p t o", p=P))
+        make_identity(nc, ident[:])
+        nc.gpsimd.dma_start(out=w3w[:].bitcast(I32), in_=w3_words[0].bitcast(I32))
+        load_scales(nc.sync, w3s, w3_scales)
+
+        xg = sb("xg", S, U32)
+        xgs = sb("xgs", S, U8)
+        nc.vector.tensor_copy(out=xgs[:], in_=xs[:].indirect(offs_sb[:]))
+        nc.vector.tensor_copy(out=xg[:], in_=xw[:].indirect(offs_sb[:]))
+
+        def product(acc, words, scales, t):
+            nc.tensor.matmul_mx(
+                out=acc[:], lhsT=words[:, cols(t, 2 * P)].bitcast(FP4X4), lhsT_scale=scales[:, cols(t, P)],
+                rhs=xg[:].bitcast(FP8X4), rhs_scale=xgs[:], start=True, stop=True,
+            )
+
+        def turn(acc, terms):
+            for b in range(BLOCKS):
+                for i, term in enumerate(terms):
+                    nc.tensor.matmul(
+                        acc[:, cols(b, P)], lhsT=term[:, cols(b, P)], rhs=ident[:],
+                        start=(i == 0), stop=(i == len(terms) - 1), is_transpose=True,
+                    )
+
+        def tiles(name, dtype=F32):
+            return [sb("%s%d" % (name, t), S, dtype) for t in range(TILES)]
+
+        def fetch_vector(dst, window, lst):
+            for h in range(2):
+                nc.vector.tensor_copy(out=dst[:, cols(h, HALF)], in_=window[:].indirect(half_of(lst, h)))
+
+        th, ft, s1, s2, a1, a2 = (tiles(n) for n in ("th", "ft", "s1_", "s2_", "a1_", "a2_"))
+        cross, us1, ncs, fb, nfa = (tiles(n) for n in ("cross", "us1_", "ncs", "fb", "nfa"))
+        den_sq, wgt, pull = (tiles(n) for n in ("den_sq", "wgt", "pull"))
+        prod = keep.tile([P, TILES * S], F32, name="prod", tag="prod_then_inv", align_bytes=64)
+        hid_t = sb("hid_t", BLOCKS * H, BF16)
+        hid = [sb("hid%d" % h, 4 * HALF, BF16) for h in range(2)]
+        codes = [sb("codes%d" % h, HALF, U32) for h in range(2)]
+        hscale = [sb("hscale%d" % h, HALF, U8) for h in range(2)]
+        shaded = [sb("shaded%d" % m, S) for m in range(N // P)]
+        result = [sb("result%d" % m, S) for m in range(N // P)]
+        ft_acc, den, a2t, diff, base = {}, {}, {}, {}, {}
+        for t in range(TILES):
+            sd_acc = bank(t, "sd_acc%d" % t)
+            product(sd_acc, w2w, w2s, t)
+            nc.scalar.activation(out=th[t][:], in_=sd_acc[:], func=ACT.Tanh)
+        for t in range(TILES):
+            ft_acc[t] = bank(TILES + t, "ft_acc%d" % t)
+            product(ft_acc[t], w1w, w1s, t)
+
+        def ends(t):
+            fetch_vector(s1[t], th[t], e1_sb)
+            fetch_vector(s2[t], th[t], e2_sb)
+            nc.gpsimd.tensor_tensor(out=prod[:, cols(t, S)], in0=s1[t][:], in1=s2[t][:], op=ALU.mult)
+
+        def sizes(t):
+            nc.scalar.activation(out=a1[t][:], in_=s1[t][:], func=ACT.Abs)
+            nc.scalar.activation(out=a2[t][:], in_=s2[t][:], func=ACT.Abs)
+            den[t] = bank(t, "den%d" % t)
+            turn(den[t], [a1[t], a2[t]])
+
+        def features(t):
+            if t < SCALAR_FEATURE_TILES:
+                nc.scalar.activation(out=ft[t][:], in_=ft_acc[t][:], func=ACT.Copy, scale=unit_sb[:, t : t + 1])
+            else:
+                nc.vector.tensor_scalar(out=ft[t][:], in0=ft_acc[t][:], scalar1=unit_sb[:, t : t + 1], scalar2=None, op0=ALU.mult)
+            a2t[t] = bank(TILES + t, "a2t%d" % t)
+            turn(a2t[t], [a2[t]])
+
+        def crossing(t):
+            nc.scalar.activation(out=cross[t][:], in_=prod[:, cols(t, S)], func=ACT.Sigmoid, scale=-4.0)
+            nc.gpsimd.tensor_scalar(out=us1[t][:], in0=s1[t][:], scalar1=unit_sb[:, t : t + 1], scalar2=-1.0, op0=ALU.mult, op1=ALU.mult)
+            nc.gpsimd.tensor_tensor(out=ncs[t][:], in0=cross[t][:], in1=us1[t][:], op=ALU.mult)
+
+        def square(t):
+            nc.scalar.activation(out=den_sq[t][:], in_=den[t][:], func=ACT.Square, bias=0.2)
+
+        def invert(t):
+            nc.scalar.activation(out=inv[:, cols(t, S)], in_=den_sq[t][:], func=ACT.Abs_reciprocal_sqrt)
+
+        def first_end(t):
+            for h in range(2):
+                nc.scalar.activation(out=nfa[t][:, cols(h, HALF)], in_=ft[t][:].indirect(half_of(e1_sb, h)), func=ACT.Copy, scale=-1.0)
+
+        def second_end(t):
+            fetch_vector(fb[t], ft[t], e2_sb)
+
+        def difference(t):
+            diff[t] = bank(t, "diff%d" % t)
+            turn(diff[t], [nfa[t], fb[t]])
+
+        def weight(t):
+            nc.vector.scalar_tensor_tensor(out=wgt[t][:], in0=a2t[t][:], scalar=0.1, in1=inv[:, cols(t, S)], op0=ALU.add, op1=ALU.mult)
+            base[t] = bank(TILES + t, "base%d" % t)
+            turn(base[t], [ncs[t], fb[t]])
+
+        def shift(t, c=slice(0, S)):
+            nc.vector.tensor_tensor(out=pull[t][:, c], in0=diff[t][:, c], in1=wgt[t][:, c], op=ALU.mult)
+
+        def hidden(t):
+            nc.vector.tensor_tensor(
+                out=hid_t[:].rearrange("p (b f) -> p b f", f=H)[:, :, cols(t, P)],
+                in0=base[t][:].rearrange("p (b f) -> p b f", f=P),
+                in1=pull[t][:].rearrange("p (b f) -> p b f", f=P), op=ALU.subtract,
+            )
+
+        def hidden_block(t, b):
+            nc.vector.tensor_tensor(
+                out=hid_t[:, b * H + t * P : b * H + (t + 1) * P], in0=base[t][:, cols(b, P)], in1=pull[t][:, cols(b, P)], op=ALU.subtract
+            )
+
+        def turn_back(b, slot, copy):
+            back = bank(slot, "back%d" % b)
+            words = hid_t[:, cols(b, H)].bitcast(F32)
+            for u in range(2):
+                nc.tensor.transpose(back[:, cols(u, P)], words[:, u : 2 * P : 2], ident[:])
+            copy(
+                out=hid[b // 2][:, cols(b % 2, 4 * P)].bitcast(F32).rearrange("p (j u) -> p j u", u=2),
+                in_=back[:, 0 : 2 * P].rearrange("p (u j) -> p j u", u=2),
+            )
+
+        def shade(h, slots, copies):
+            nc.vector.quantize_mx(out=codes[h][:].bitcast(FP8X4), scales=hscale[h][:], in_=hid[h][:])
+            for m in range(N // P):
+                acc = bank(slots[m], "shade%d_%d" % (m, h))
+                nc.tensor.matmul_mx(
+                    out=acc[:, 0:HALF], lhsT=w3w[:, cols(m, 2 * P)].bitcast(FP4X4), lhsT_scale=w3s[:, cols(m, P)],
+                    rhs=codes[h][:].bitcast(FP8X4), rhs_scale=hscale[h][:], start=True, stop=True,
+                )
+                copies[m](out=shaded[m][:, cols(h, HALF)], in_=acc[:, 0:HALF])
+
+        ends(0)
+        sizes(0)
+        features(0)
+        ends(1)
+        sizes(1)
+        features(1)
+        crossing(0)
+        square(0)
+        ends(2)
+        sizes(2)
+        crossing(1)
+        ends(3)
+        crossing(2)
+        square(1)
+        sizes(3)
+        features(2)
+        features(3)
+        first_end(0)
+        crossing(3)
+        second_end(0)
+        difference(0)
+        inv = keep.tile([P, TILES * S], F32, name="inv", tag="prod_then_inv", align_bytes=64)
+        invert(0)
+        invert(1)
+        first_end(1)
+        second_end(1)
+        difference(1)
+        second_end(2)
+        weight(0)
+        shift(0)
+        square(2)
+        invert(2)
+        first_end(2)
+        difference(2)
+        weight(1)
+        hidden(0)
+        shift(1)
+        second_end(3)
+        square(3)
+        invert(3)
+        first_end(3)
+        difference(3)
+        hidden(1)
+        weight(2)
+        shift(2)
+        weight(3)
+        hidden(2)
+        last = TILES - 1
+        for b in range(BLOCKS):
+            shift(last, cols(b, P))
+        for b in range(BLOCKS):
+            hidden_block(last, b)
+        turn_back(0, 0, nc.scalar.copy)
+        turn_back(1, 1, nc.scalar.copy)
+        turn_back(2, 2, nc.vector.tensor_copy)
+        turn_back(3, 4, nc.scalar.copy)
+        shade(0, (5, 6), (nc.scalar.copy, nc.scalar.copy))
+        shade(1, (0, 1), (nc.vector.tensor_copy, nc.scalar.copy))
+
+        for h in range(2):
+            c = cols(h, HALF)
+            nc.vector.tensor_copy(out=result[0][:, c], in_=shaded[0][:].indirect(half_of(fc_sb, h)))
+            nc.sync.dma_start(out=out[0:P, c], in_=result[0][:, c])
+            nc.scalar.activation(out=result[1][:, c], in_=shaded[1][:].indirect(half_of(fc_sb, h)), func=ACT.Copy)
+            nc.sync.dma_start(out=out[P : 2 * P, c], in_=result[1][:, c])

@@ -23,6 +23,7 @@ BLOCKS = S // P
 HALF = S // 2
 LIST_COLS = S // 16
 SCALAR_FEATURE_TILES = 2
+PRESUMMED = (2, 3,)
 
 
 def tile_picked_ymarch_off_p_kernel(
@@ -71,13 +72,13 @@ def tile_picked_ymarch_off_p_kernel(
         nc.gpsimd.dma_start(out=w2w[:].bitcast(I32), in_=w2_words[0].bitcast(I32))
         nc.sync.dma_start(out=offs_sb[:], in_=offs)
         nc.sync.dma_start(out=xw[:].bitcast(I32), in_=x_words[0].rearrange("p n t -> p (n t)").bitcast(I32))
-        load_scales(nc.scalar, xs, x_scales)
-        load_scales(nc.scalar, w2s, w2_scales)
+        load_scales(nc.sync, xs, x_scales)
+        load_scales(nc.sync, w2s, w2_scales)
+        nc.gpsimd.dma_start(out=w1w[:].bitcast(I32), in_=w1_words[0].bitcast(I32))
+        load_scales(nc.sync, w1s, w1_scales)
         nc.sync.dma_start(out=e1_sb[:], in_=e1)
         nc.sync.dma_start(out=e2_sb[:], in_=e2)
         nc.sync.dma_start(out=fc_sb[:], in_=fc)
-        nc.gpsimd.dma_start(out=w1w[:].bitcast(I32), in_=w1_words[0].bitcast(I32))
-        load_scales(nc.sync, w1s, w1_scales)
         with nc.allow_non_contiguous_dma(reason="one value a partition"):
             nc.gpsimd.dma_start(out=unit_sb[:].rearrange("p (t o) -> p t o", o=1), in_=unit.rearrange("(t p) o -> p t o", p=P))
         make_identity(nc, ident[:])
@@ -86,22 +87,31 @@ def tile_picked_ymarch_off_p_kernel(
 
         xg = sb("xg", S, U32)
         xgs = sb("xgs", S, U8)
-        nc.vector.tensor_copy(out=xgs[:], in_=xs[:].indirect(offs_sb[:]))
         nc.vector.tensor_copy(out=xg[:], in_=xw[:].indirect(offs_sb[:]))
+        for h in range(2):
+            nc.vector.tensor_copy(out=xgs[:, cols(h, HALF)], in_=xs[:].indirect(half_of(offs_sb, h)))
 
-        def product(acc, words, scales, t):
+        half_unit = sb("half_unit", TILES)
+        neg_half_unit = sb("neg_half_unit", TILES)
+        nc.gpsimd.tensor_scalar(out=half_unit[:], in0=unit_sb[:], scalar1=0.5, scalar2=0.0, op0=ALU.mult, op1=ALU.add)
+        nc.gpsimd.tensor_scalar(out=neg_half_unit[:], in0=unit_sb[:], scalar1=-0.5, scalar2=0.0, op0=ALU.mult, op1=ALU.add)
+
+        def product(acc, words, scales, t, c=slice(0, S)):
             nc.tensor.matmul_mx(
-                out=acc[:], lhsT=words[:, cols(t, 2 * P)].bitcast(FP4X4), lhsT_scale=scales[:, cols(t, P)],
-                rhs=xg[:].bitcast(FP8X4), rhs_scale=xgs[:], start=True, stop=True,
+                out=acc[:, c], lhsT=words[:, cols(t, 2 * P)].bitcast(FP4X4), lhsT_scale=scales[:, cols(t, P)],
+                rhs=xg[:, c].bitcast(FP8X4), rhs_scale=xgs[:, c], start=True, stop=True,
             )
 
-        def turn(acc, terms):
-            for b in range(BLOCKS):
-                for i, term in enumerate(terms):
-                    nc.tensor.matmul(
-                        acc[:, cols(b, P)], lhsT=term[:, cols(b, P)], rhs=ident[:],
-                        start=(i == 0), stop=(i == len(terms) - 1), is_transpose=True,
-                    )
+        def cells(u):
+            pair, h = divmod(u, 2)
+            return [(2 * pair + i, 2 * h + j, cols(2 * j + i, P)) for i in range(2) for j in range(2)]
+
+        def turn(acc_cols, terms, b):
+            for i, term in enumerate(terms):
+                nc.tensor.matmul(
+                    acc_cols, lhsT=term[:, cols(b, P)], rhs=ident[:],
+                    start=(i == 0), stop=(i == len(terms) - 1), is_transpose=True,
+                )
 
         def tiles(name, dtype=F32):
             return [sb("%s%d" % (name, t), S, dtype) for t in range(TILES)]
@@ -111,7 +121,7 @@ def tile_picked_ymarch_off_p_kernel(
                 nc.vector.tensor_copy(out=dst[:, cols(h, HALF)], in_=window[:].indirect(half_of(lst, h)))
 
         th, ft, s1, s2, a1, a2 = (tiles(n) for n in ("th", "ft", "s1_", "s2_", "a1_", "a2_"))
-        cross, us1, ncs, fb, nfa = (tiles(n) for n in ("cross", "us1_", "ncs", "fb", "nfa"))
+        tp, gate, ncs, fb, nfa, fixed = (tiles(n) for n in ("tp", "gate", "ncs", "fb", "nfa", "fixed"))
         den_sq, wgt, pull = (tiles(n) for n in ("den_sq", "wgt", "pull"))
         prod = keep.tile([P, TILES * S], F32, name="prod", tag="prod_then_inv", align_bytes=64)
         hid_t = sb("hid_t", BLOCKS * H, BF16)
@@ -123,8 +133,9 @@ def tile_picked_ymarch_off_p_kernel(
         ft_acc, den, a2t, diff, base = {}, {}, {}, {}, {}
         for t in range(TILES):
             sd_acc = bank(t, "sd_acc%d" % t)
-            product(sd_acc, w2w, w2s, t)
-            nc.scalar.activation(out=th[t][:], in_=sd_acc[:], func=ACT.Tanh)
+            for c in [cols(h, HALF) for h in range(2)] if t == 0 else [slice(0, S)]:
+                product(sd_acc, w2w, w2s, t, c)
+                nc.scalar.activation(out=th[t][:, c], in_=sd_acc[:, c], func=ACT.Tanh)
         for t in range(TILES):
             ft_acc[t] = bank(TILES + t, "ft_acc%d" % t)
             product(ft_acc[t], w1w, w1s, t)
@@ -137,27 +148,41 @@ def tile_picked_ymarch_off_p_kernel(
         def sizes(t):
             nc.scalar.activation(out=a1[t][:], in_=s1[t][:], func=ACT.Abs)
             nc.scalar.activation(out=a2[t][:], in_=s2[t][:], func=ACT.Abs)
-            den[t] = bank(t, "den%d" % t)
-            turn(den[t], [a1[t], a2[t]])
+            for u in (t // 2 * 2, t // 2 * 2 + 1):
+                if t % 2 == 0:
+                    den[u] = bank(u, "den%d" % u)
+                for tt, b, c in cells(u):
+                    if tt == t:
+                        turn(den[u][:, c], [a1[t], a2[t]], b)
 
         def features(t):
             if t < SCALAR_FEATURE_TILES:
                 nc.scalar.activation(out=ft[t][:], in_=ft_acc[t][:], func=ACT.Copy, scale=unit_sb[:, t : t + 1])
             else:
                 nc.vector.tensor_scalar(out=ft[t][:], in0=ft_acc[t][:], scalar1=unit_sb[:, t : t + 1], scalar2=None, op0=ALU.mult)
-            a2t[t] = bank(TILES + t, "a2t%d" % t)
-            turn(a2t[t], [a2[t]])
+
+        def second_size(u):
+            a2t[u] = bank(TILES + u, "a2t%d" % u)
+            for t, b, c in cells(u):
+                turn(a2t[u][:, c], [a2[t]], b)
 
         def crossing(t):
-            nc.scalar.activation(out=cross[t][:], in_=prod[:, cols(t, S)], func=ACT.Sigmoid, scale=-4.0)
-            nc.gpsimd.tensor_scalar(out=us1[t][:], in0=s1[t][:], scalar1=unit_sb[:, t : t + 1], scalar2=-1.0, op0=ALU.mult, op1=ALU.mult)
-            nc.gpsimd.tensor_tensor(out=ncs[t][:], in0=cross[t][:], in1=us1[t][:], op=ALU.mult)
+            nc.scalar.activation(out=tp[t][:], in_=prod[:, cols(t, S)], func=ACT.Tanh, scale=2.0)
 
-        def square(t):
-            nc.scalar.activation(out=den_sq[t][:], in_=den[t][:], func=ACT.Square, bias=0.2)
+        def crossed(t):
+            nc.gpsimd.tensor_scalar(
+                out=gate[t][:], in0=tp[t][:], scalar1=half_unit[:, t : t + 1], scalar2=neg_half_unit[:, t : t + 1], op0=ALU.mult, op1=ALU.add
+            )
+            nc.gpsimd.tensor_tensor(out=ncs[t][:], in0=gate[t][:], in1=s1[t][:], op=ALU.mult)
 
-        def invert(t):
-            nc.scalar.activation(out=inv[:, cols(t, S)], in_=den_sq[t][:], func=ACT.Abs_reciprocal_sqrt)
+        def presum(t):
+            nc.gpsimd.tensor_tensor(out=fixed[t][:], in0=ncs[t][:], in1=fb[t][:], op=ALU.add)
+
+        def square(u):
+            nc.scalar.activation(out=den_sq[u][:], in_=den[u][:], func=ACT.Square, bias=0.2)
+
+        def invert(u):
+            nc.scalar.activation(out=inv[:, cols(u, S)], in_=den_sq[u][:], func=ACT.Abs_reciprocal_sqrt)
 
         def first_end(t):
             for h in range(2):
@@ -166,29 +191,35 @@ def tile_picked_ymarch_off_p_kernel(
         def second_end(t):
             fetch_vector(fb[t], ft[t], e2_sb)
 
-        def difference(t):
-            diff[t] = bank(t, "diff%d" % t)
-            turn(diff[t], [nfa[t], fb[t]])
+        def difference(u):
+            diff[u] = bank(u, "diff%d" % u)
+            for t, b, c in cells(u):
+                turn(diff[u][:, c], [nfa[t], fb[t]], b)
 
-        def weight(t):
-            nc.vector.scalar_tensor_tensor(out=wgt[t][:], in0=a2t[t][:], scalar=0.1, in1=inv[:, cols(t, S)], op0=ALU.add, op1=ALU.mult)
-            base[t] = bank(TILES + t, "base%d" % t)
-            turn(base[t], [ncs[t], fb[t]])
+        def weight(u):
+            nc.vector.scalar_tensor_tensor(out=wgt[u][:], in0=a2t[u][:], scalar=0.1, in1=inv[:, cols(u, S)], op0=ALU.add, op1=ALU.mult)
+            base[u] = bank(TILES + u, "base%d" % u)
+            for t, b, c in cells(u):
+                turn(base[u][:, c], [fixed[t]] if t in PRESUMMED else [ncs[t], fb[t]], b)
 
-        def shift(t, c=slice(0, S)):
-            nc.vector.tensor_tensor(out=pull[t][:, c], in0=diff[t][:, c], in1=wgt[t][:, c], op=ALU.mult)
+        def shift(u, parts=1):
+            for i in range(parts):
+                c = cols(i, S // parts)
+                nc.vector.tensor_tensor(out=pull[u][:, c], in0=diff[u][:, c], in1=wgt[u][:, c], op=ALU.mult)
 
-        def hidden(t):
-            nc.vector.tensor_tensor(
-                out=hid_t[:].rearrange("p (b f) -> p b f", f=H)[:, :, cols(t, P)],
-                in0=base[t][:].rearrange("p (b f) -> p b f", f=P),
-                in1=pull[t][:].rearrange("p (b f) -> p b f", f=P), op=ALU.subtract,
-            )
-
-        def hidden_block(t, b):
-            nc.vector.tensor_tensor(
-                out=hid_t[:, b * H + t * P : b * H + (t + 1) * P], in0=base[t][:, cols(b, P)], in1=pull[t][:, cols(b, P)], op=ALU.subtract
-            )
+        def hidden(u, parts=1):
+            pair, h = divmod(u, 2)
+            dst = hid_t[:].rearrange("p (b f) -> p b f", f=H)[:, 2 * h : 2 * h + 2, cols(pair, 2 * P)]
+            if parts == 1:
+                nc.vector.tensor_tensor(
+                    out=dst, in0=base[u][:].rearrange("p (b f) -> p b f", b=2), in1=pull[u][:].rearrange("p (b f) -> p b f", b=2), op=ALU.subtract
+                )
+            else:
+                for j in range(2):
+                    first = (2 * h + j) * H + pair * 2 * P
+                    nc.vector.tensor_tensor(
+                        out=hid_t[:, first : first + 2 * P], in0=base[u][:, cols(j, HALF)], in1=pull[u][:, cols(j, HALF)], op=ALU.subtract
+                    )
 
         def turn_back(b, slot, copy):
             back = bank(slot, "back%d" % b)
@@ -217,56 +248,63 @@ def tile_picked_ymarch_off_p_kernel(
         sizes(1)
         features(1)
         crossing(0)
-        square(0)
+        crossed(0)
+        second_size(0)
+        second_size(1)
         ends(2)
+        square(0)
         sizes(2)
         crossing(1)
+        crossed(1)
         ends(3)
-        crossing(2)
         square(1)
+        crossing(2)
+        crossed(2)
         sizes(3)
         features(2)
         features(3)
+        second_size(2)
+        second_size(3)
         first_end(0)
         crossing(3)
+        crossed(3)
         second_end(0)
-        difference(0)
+        second_end(1)
         inv = keep.tile([P, TILES * S], F32, name="inv", tag="prod_then_inv", align_bytes=64)
         invert(0)
-        invert(1)
         first_end(1)
-        second_end(1)
+        difference(0)
         difference(1)
+        invert(1)
         second_end(2)
+        second_end(3)
         weight(0)
         shift(0)
         square(2)
         invert(2)
         first_end(2)
-        difference(2)
+        presum(2)
+        presum(3)
         weight(1)
         hidden(0)
         shift(1)
-        second_end(3)
+        first_end(3)
+        difference(2)
         square(3)
         invert(3)
-        first_end(3)
         difference(3)
         hidden(1)
         weight(2)
-        shift(2)
         weight(3)
+        shift(2)
         hidden(2)
-        last = TILES - 1
-        for b in range(BLOCKS):
-            shift(last, cols(b, P))
-        for b in range(BLOCKS):
-            hidden_block(last, b)
+        shift(3,2)
         turn_back(0, 0, nc.scalar.copy)
         turn_back(1, 1, nc.scalar.copy)
-        turn_back(2, 2, nc.vector.tensor_copy)
-        turn_back(3, 4, nc.scalar.copy)
-        shade(0, (5, 6), (nc.scalar.copy, nc.scalar.copy))
+        hidden(3,2)
+        turn_back(2, 2, nc.scalar.copy)
+        turn_back(3, 6, nc.scalar.copy)
+        shade(0, (4, 5), (nc.scalar.copy, nc.scalar.copy))
         shade(1, (0, 1), (nc.vector.tensor_copy, nc.scalar.copy))
 
         for h in range(2):

@@ -18,12 +18,17 @@ ACT = mybir.ActivationFunctionType
 ALU = mybir.AluOpType
 
 P = 128
+PACK = 4
 TILES = H // P
 BLOCKS = S // P
+QUARTERS = 4
+OUT_TILES = N // P
 HALF = S // 2
 LIST_COLS = S // 16
-SCALAR_FEATURE_TILES = 2
-PRESUMMED = (2, 3,)
+BANKS = 8
+SCALAR_FT_TILES = 2
+EARLY_FA_QUARTERS = 1
+PIECES = ((0, 1), (2,), (3,))
 
 
 def tile_picked_ymarch_off_p_kernel(
@@ -37,6 +42,9 @@ def tile_picked_ymarch_off_p_kernel(
         def sb(name, width, dtype=F32):
             return keep.tile([P, width], dtype, name=name, align_bytes=64)
 
+        def four(name):
+            return [sb("%s%d" % (name, i), S) for i in range(4)]
+
         def bank(slot, name):
             return psum.tile([P, S], F32, name=name, tag="bank%d" % slot)
 
@@ -46,9 +54,9 @@ def tile_picked_ymarch_off_p_kernel(
         def half_of(lst, h):
             return lst[:, cols(h, LIST_COLS // 2)]
 
-        def load_scales(queue, tile_cols, src):
+        def load_scales(plane, src):
             for q in range(4):
-                queue.dma_start(out=tile_cols[32 * q : 32 * q + 4, :].bitcast(I32), in_=src[0, 4 * q : 4 * q + 4, :].bitcast(I32))
+                nc.sync.dma_start(out=plane[32 * q : 32 * q + 4, :].bitcast(I32), in_=src[0, 4 * q : 4 * q + 4, :].bitcast(I32))
 
         offs_sb = keep.tile([P, LIST_COLS], U16, name="offs_sb")
         e1_sb = keep.tile([P, LIST_COLS], U16, name="e1_sb")
@@ -65,25 +73,23 @@ def tile_picked_ymarch_off_p_kernel(
         unit_sb = sb("unit_sb", TILES)
         ident = sb("ident", P)
 
-        nc.vector.memset(xs[:].bitcast(I32), 0)
-        nc.vector.memset(w2s[:].bitcast(I32), 0)
-        nc.vector.memset(w1s[:].bitcast(I32), 0)
-        nc.vector.memset(w3s[:].bitcast(I32), 0)
+        for plane in (xs, w2s, w1s, w3s):
+            nc.vector.memset(plane[:].bitcast(I32), 0)
         nc.gpsimd.dma_start(out=w2w[:].bitcast(I32), in_=w2_words[0].bitcast(I32))
         nc.sync.dma_start(out=offs_sb[:], in_=offs)
         nc.sync.dma_start(out=xw[:].bitcast(I32), in_=x_words[0].rearrange("p n t -> p (n t)").bitcast(I32))
-        load_scales(nc.sync, xs, x_scales)
-        load_scales(nc.sync, w2s, w2_scales)
+        load_scales(xs, x_scales)
+        load_scales(w2s, w2_scales)
         nc.gpsimd.dma_start(out=w1w[:].bitcast(I32), in_=w1_words[0].bitcast(I32))
-        load_scales(nc.sync, w1s, w1_scales)
+        load_scales(w1s, w1_scales)
         nc.sync.dma_start(out=e1_sb[:], in_=e1)
         nc.sync.dma_start(out=e2_sb[:], in_=e2)
         nc.sync.dma_start(out=fc_sb[:], in_=fc)
-        with nc.allow_non_contiguous_dma(reason="one value a partition"):
+        with nc.allow_non_contiguous_dma(reason="one value of unit for each partition and tile"):
             nc.gpsimd.dma_start(out=unit_sb[:].rearrange("p (t o) -> p t o", o=1), in_=unit.rearrange("(t p) o -> p t o", p=P))
         make_identity(nc, ident[:])
         nc.gpsimd.dma_start(out=w3w[:].bitcast(I32), in_=w3_words[0].bitcast(I32))
-        load_scales(nc.sync, w3s, w3_scales)
+        load_scales(w3s, w3_scales)
 
         xg = sb("xg", S, U32)
         xgs = sb("xgs", S, U8)
@@ -91,221 +97,229 @@ def tile_picked_ymarch_off_p_kernel(
         for h in range(2):
             nc.vector.tensor_copy(out=xgs[:, cols(h, HALF)], in_=xs[:].indirect(half_of(offs_sb, h)))
 
-        half_unit = sb("half_unit", TILES)
-        neg_half_unit = sb("neg_half_unit", TILES)
-        nc.gpsimd.tensor_scalar(out=half_unit[:], in0=unit_sb[:], scalar1=0.5, scalar2=0.0, op0=ALU.mult, op1=ALU.add)
-        nc.gpsimd.tensor_scalar(out=neg_half_unit[:], in0=unit_sb[:], scalar1=-0.5, scalar2=0.0, op0=ALU.mult, op1=ALU.add)
-
-        def product(acc, words, scales, t, c=slice(0, S)):
+        def corner_product(acc, words, scales, t, c):
             nc.tensor.matmul_mx(
-                out=acc[:, c], lhsT=words[:, cols(t, 2 * P)].bitcast(FP4X4), lhsT_scale=scales[:, cols(t, P)],
-                rhs=xg[:, c].bitcast(FP8X4), rhs_scale=xgs[:, c], start=True, stop=True,
+                out=acc[:, c],
+                lhsT=words[:, cols(t, 2 * P)].bitcast(FP4X4),
+                lhsT_scale=scales[:, cols(t, P)],
+                rhs=xg[:, c].bitcast(FP8X4),
+                rhs_scale=xgs[:, c],
+                start=True,
+                stop=True,
             )
 
+        th, ft, s1, s2, abs1, abs2 = (four(n) for n in ("th", "ft", "s1_", "s2_", "abs1_", "abs2_"))
+        cross, neg_us1, neg_cs, fb, neg_fa, fixed = (four(n) for n in ("cross", "neg_us1_", "neg_cs", "fb", "neg_fa", "fixed"))
+        den_sq, weight, pull = (four(n) for n in ("den_sq", "weight", "pull"))
+        prod = keep.tile([P, TILES * S], F32, name="prod", tag="prod_then_inv", align_bytes=64)
+        hid_turned = sb("hid_turned", BLOCKS * H, BF16)
+        shaded = [sb("shaded%d" % m, S) for m in range(OUT_TILES)]
+        result = [sb("result%d" % m, S) for m in range(OUT_TILES)]
+        ft_acc, den, abs2_turned, diff, fixed_turned = {}, {}, {}, {}, {}
+
+        whole = slice(0, S)
+        sd_acc = bank(0, "sd_acc0")
+        first_sigmoid = sb("first_sigmoid", HALF)
+        corner_product(sd_acc, w2w, w2s, 0, cols(0, HALF))
+        nc.scalar.activation(out=first_sigmoid[:], in_=sd_acc[:, cols(0, HALF)], func=ACT.Sigmoid, scale=2.0)
+        nc.scalar.activation(out=th[0][:, cols(0, HALF)], in_=first_sigmoid[:], func=ACT.Identity, scale=2.0, bias=-1.0)
+        corner_product(sd_acc, w2w, w2s, 0, cols(1, HALF))
+        nc.scalar.activation(out=th[0][:, cols(1, HALF)], in_=sd_acc[:, cols(1, HALF)], func=ACT.Tanh)
+        for t in range(1, TILES):
+            sd_acc = bank(t, "sd_acc%d" % t)
+            corner_product(sd_acc, w2w, w2s, t, whole)
+            nc.scalar.activation(out=th[t][:], in_=sd_acc[:], func=ACT.Tanh)
+        for t in range(TILES):
+            ft_acc[t] = bank(TILES + t, "ft_acc%d" % t)
+            corner_product(ft_acc[t], w1w, w1s, t, whole)
+
+        def quarter_tiles(u):
+            return (u // 2 * 2, u // 2 * 2 + 1)
+
         def cells(u):
-            pair, h = divmod(u, 2)
-            return [(2 * pair + i, 2 * h + j, cols(2 * j + i, P)) for i in range(2) for j in range(2)]
+            return [(t, u % 2 * 2 + j, cols(2 * j + t % 2, P)) for t in quarter_tiles(u) for j in range(2)]
 
         def turn(acc_cols, terms, b):
             for i, term in enumerate(terms):
                 nc.tensor.matmul(
-                    acc_cols, lhsT=term[:, cols(b, P)], rhs=ident[:],
-                    start=(i == 0), stop=(i == len(terms) - 1), is_transpose=True,
+                    acc_cols,
+                    lhsT=term[:, cols(b, P)],
+                    rhs=ident[:],
+                    start=(i == 0),
+                    stop=(i == len(terms) - 1),
+                    is_transpose=True,
                 )
 
-        def tiles(name, dtype=F32):
-            return [sb("%s%d" % (name, t), S, dtype) for t in range(TILES)]
-
-        def fetch_vector(dst, window, lst):
-            for h in range(2):
-                nc.vector.tensor_copy(out=dst[:, cols(h, HALF)], in_=window[:].indirect(half_of(lst, h)))
-
-        th, ft, s1, s2, a1, a2 = (tiles(n) for n in ("th", "ft", "s1_", "s2_", "a1_", "a2_"))
-        tp, gate, ncs, fb, nfa, fixed = (tiles(n) for n in ("tp", "gate", "ncs", "fb", "nfa", "fixed"))
-        den_sq, wgt, pull = (tiles(n) for n in ("den_sq", "wgt", "pull"))
-        prod = keep.tile([P, TILES * S], F32, name="prod", tag="prod_then_inv", align_bytes=64)
-        hid_t = sb("hid_t", BLOCKS * H, BF16)
-        hid = [sb("hid%d" % h, 4 * HALF, BF16) for h in range(2)]
-        codes = [sb("codes%d" % h, HALF, U32) for h in range(2)]
-        hscale = [sb("hscale%d" % h, HALF, U8) for h in range(2)]
-        shaded = [sb("shaded%d" % m, S) for m in range(N // P)]
-        result = [sb("result%d" % m, S) for m in range(N // P)]
-        ft_acc, den, a2t, diff, base = {}, {}, {}, {}, {}
-        for t in range(TILES):
-            sd_acc = bank(t, "sd_acc%d" % t)
-            for c in [cols(h, HALF) for h in range(2)] if t == 0 else [slice(0, S)]:
-                product(sd_acc, w2w, w2s, t, c)
-                nc.scalar.activation(out=th[t][:, c], in_=sd_acc[:, c], func=ACT.Tanh)
-        for t in range(TILES):
-            ft_acc[t] = bank(TILES + t, "ft_acc%d" % t)
-            product(ft_acc[t], w1w, w1s, t)
-
-        def ends(t):
-            fetch_vector(s1[t], th[t], e1_sb)
-            fetch_vector(s2[t], th[t], e2_sb)
+        def fetch_signs(t):
+            for dst, lst in ((s1[t], e1_sb), (s2[t], e2_sb)):
+                for h in range(2):
+                    nc.vector.tensor_copy(out=dst[:, cols(h, HALF)], in_=th[t][:].indirect(half_of(lst, h)))
             nc.gpsimd.tensor_tensor(out=prod[:, cols(t, S)], in0=s1[t][:], in1=s2[t][:], op=ALU.mult)
 
-        def sizes(t):
-            nc.scalar.activation(out=a1[t][:], in_=s1[t][:], func=ACT.Abs)
-            nc.scalar.activation(out=a2[t][:], in_=s2[t][:], func=ACT.Abs)
-            for u in (t // 2 * 2, t // 2 * 2 + 1):
+        def sum_magnitudes(t):
+            nc.gpsimd.tensor_scalar(
+                out=neg_us1[t][:], in0=s1[t][:], scalar1=unit_sb[:, t : t + 1], scalar2=-1.0, op0=ALU.mult, op1=ALU.mult
+            )
+            nc.scalar.activation(out=abs1[t][:], in_=s1[t][:], func=ACT.Abs)
+            nc.scalar.activation(out=abs2[t][:], in_=s2[t][:], func=ACT.Abs)
+            for u in quarter_tiles(t):
                 if t % 2 == 0:
                     den[u] = bank(u, "den%d" % u)
-                for tt, b, c in cells(u):
-                    if tt == t:
-                        turn(den[u][:, c], [a1[t], a2[t]], b)
+                for cell_tile, b, c in cells(u):
+                    if cell_tile == t:
+                        turn(den[u][:, c], [abs1[t], abs2[t]], b)
 
-        def features(t):
-            if t < SCALAR_FEATURE_TILES:
+        def scale_features(t):
+            if t < SCALAR_FT_TILES:
                 nc.scalar.activation(out=ft[t][:], in_=ft_acc[t][:], func=ACT.Copy, scale=unit_sb[:, t : t + 1])
             else:
                 nc.vector.tensor_scalar(out=ft[t][:], in0=ft_acc[t][:], scalar1=unit_sb[:, t : t + 1], scalar2=None, op0=ALU.mult)
 
-        def second_size(u):
-            a2t[u] = bank(TILES + u, "a2t%d" % u)
-            for t, b, c in cells(u):
-                turn(a2t[u][:, c], [a2[t]], b)
-
         def crossing(t):
-            nc.scalar.activation(out=tp[t][:], in_=prod[:, cols(t, S)], func=ACT.Tanh, scale=2.0)
+            nc.scalar.activation(out=cross[t][:], in_=prod[:, cols(t, S)], func=ACT.Sigmoid, scale=-4.0)
 
-        def crossed(t):
-            nc.gpsimd.tensor_scalar(
-                out=gate[t][:], in0=tp[t][:], scalar1=half_unit[:, t : t + 1], scalar2=neg_half_unit[:, t : t + 1], op0=ALU.mult, op1=ALU.add
-            )
-            nc.gpsimd.tensor_tensor(out=ncs[t][:], in0=gate[t][:], in1=s1[t][:], op=ALU.mult)
+        def weigh_crossing(t):
+            nc.gpsimd.tensor_tensor(out=neg_cs[t][:], in0=cross[t][:], in1=neg_us1[t][:], op=ALU.mult)
 
-        def presum(t):
-            nc.gpsimd.tensor_tensor(out=fixed[t][:], in0=ncs[t][:], in1=fb[t][:], op=ALU.add)
+        def turn_abs2(u):
+            abs2_turned[u] = bank(QUARTERS + u, "abs2_turned%d" % u)
+            for t, b, c in cells(u):
+                turn(abs2_turned[u][:, c], [abs2[t]], b)
 
-        def square(u):
+        def square_den(u):
             nc.scalar.activation(out=den_sq[u][:], in_=den[u][:], func=ACT.Square, bias=0.2)
 
-        def invert(u):
-            nc.scalar.activation(out=inv[:, cols(u, S)], in_=den_sq[u][:], func=ACT.Abs_reciprocal_sqrt)
+        def fetch_fb(u):
+            for t in quarter_tiles(u):
+                nc.vector.tensor_copy(out=fb[t][:, cols(u % 2, HALF)], in_=ft[t][:].indirect(half_of(e2_sb, u % 2)))
 
-        def first_end(t):
-            for h in range(2):
-                nc.scalar.activation(out=nfa[t][:, cols(h, HALF)], in_=ft[t][:].indirect(half_of(e1_sb, h)), func=ACT.Copy, scale=-1.0)
+        def fetch_neg_fa(u):
+            for t in quarter_tiles(u):
+                nc.scalar.activation(
+                    out=neg_fa[t][:, cols(u % 2, HALF)], in_=ft[t][:].indirect(half_of(e1_sb, u % 2)), func=ACT.Copy, scale=-1.0
+                )
 
-        def second_end(t):
-            fetch_vector(fb[t], ft[t], e2_sb)
+        def sum_fixed(u):
+            c = cols(u % 2, HALF)
+            for t in quarter_tiles(u):
+                nc.gpsimd.tensor_tensor(out=fixed[t][:, c], in0=neg_cs[t][:, c], in1=fb[t][:, c], op=ALU.add)
 
-        def difference(u):
+        def weigh(u):
             diff[u] = bank(u, "diff%d" % u)
             for t, b, c in cells(u):
-                turn(diff[u][:, c], [nfa[t], fb[t]], b)
-
-        def weight(u):
-            nc.vector.scalar_tensor_tensor(out=wgt[u][:], in0=a2t[u][:], scalar=0.1, in1=inv[:, cols(u, S)], op0=ALU.add, op1=ALU.mult)
-            base[u] = bank(TILES + u, "base%d" % u)
+                turn(diff[u][:, c], [neg_fa[t], fb[t]], b)
+            nc.vector.scalar_tensor_tensor(
+                out=weight[u][:], in0=abs2_turned[u][:], scalar=0.1, in1=inv[:, cols(u, S)], op0=ALU.add, op1=ALU.mult
+            )
+            fixed_turned[u] = bank(QUARTERS + u, "fixed_turned%d" % u)
             for t, b, c in cells(u):
-                turn(base[u][:, c], [fixed[t]] if t in PRESUMMED else [ncs[t], fb[t]], b)
+                turn(fixed_turned[u][:, c], [fixed[t]], b)
 
-        def shift(u, parts=1):
-            for i in range(parts):
-                c = cols(i, S // parts)
-                nc.vector.tensor_tensor(out=pull[u][:, c], in0=diff[u][:, c], in1=wgt[u][:, c], op=ALU.mult)
+        def make_pull(u, c):
+            nc.vector.tensor_tensor(out=pull[u][:, c], in0=diff[u][:, c], in1=weight[u][:, c], op=ALU.mult)
 
-        def hidden(u, parts=1):
-            pair, h = divmod(u, 2)
-            dst = hid_t[:].rearrange("p (b f) -> p b f", f=H)[:, 2 * h : 2 * h + 2, cols(pair, 2 * P)]
-            if parts == 1:
-                nc.vector.tensor_tensor(
-                    out=dst, in0=base[u][:].rearrange("p (b f) -> p b f", b=2), in1=pull[u][:].rearrange("p (b f) -> p b f", b=2), op=ALU.subtract
-                )
-            else:
-                for j in range(2):
-                    first = (2 * h + j) * H + pair * 2 * P
-                    nc.vector.tensor_tensor(
-                        out=hid_t[:, first : first + 2 * P], in0=base[u][:, cols(j, HALF)], in1=pull[u][:, cols(j, HALF)], op=ALU.subtract
-                    )
-
-        def turn_back(b, slot, copy):
-            back = bank(slot, "back%d" % b)
-            words = hid_t[:, cols(b, H)].bitcast(F32)
-            for u in range(2):
-                nc.tensor.transpose(back[:, cols(u, P)], words[:, u : 2 * P : 2], ident[:])
-            copy(
-                out=hid[b // 2][:, cols(b % 2, 4 * P)].bitcast(F32).rearrange("p (j u) -> p j u", u=2),
-                in_=back[:, 0 : 2 * P].rearrange("p (u j) -> p j u", u=2),
+        def make_hidden(u):
+            nc.vector.tensor_tensor(
+                out=hid_turned[:].rearrange("p (b f) -> p b f", f=H)[:, cols(u % 2, 2), cols(u // 2, 2 * P)],
+                in0=fixed_turned[u][:].rearrange("p (b f) -> p b f", b=2),
+                in1=pull[u][:].rearrange("p (b f) -> p b f", b=2),
+                op=ALU.subtract,
             )
 
-        def shade(h, slots, copies):
-            nc.vector.quantize_mx(out=codes[h][:].bitcast(FP8X4), scales=hscale[h][:], in_=hid[h][:])
-            for m in range(N // P):
-                acc = bank(slots[m], "shade%d_%d" % (m, h))
-                nc.tensor.matmul_mx(
-                    out=acc[:, 0:HALF], lhsT=w3w[:, cols(m, 2 * P)].bitcast(FP4X4), lhsT_scale=w3s[:, cols(m, P)],
-                    rhs=codes[h][:].bitcast(FP8X4), rhs_scale=hscale[h][:], start=True, stop=True,
-                )
-                copies[m](out=shaded[m][:, cols(h, HALF)], in_=acc[:, 0:HALF])
+        def make_hidden_block(u, j):
+            first = (u % 2 * 2 + j) * H + u // 2 * 2 * P
+            nc.vector.tensor_tensor(
+                out=hid_turned[:, first : first + 2 * P],
+                in0=fixed_turned[u][:, cols(j, HALF)],
+                in1=pull[u][:, cols(j, HALF)],
+                op=ALU.subtract,
+            )
 
-        ends(0)
-        sizes(0)
-        features(0)
-        ends(1)
-        sizes(1)
-        features(1)
-        crossing(0)
-        crossed(0)
-        second_size(0)
-        second_size(1)
-        ends(2)
-        square(0)
-        sizes(2)
-        crossing(1)
-        crossed(1)
-        ends(3)
-        square(1)
-        crossing(2)
-        crossed(2)
-        sizes(3)
-        features(2)
-        features(3)
-        second_size(2)
-        second_size(3)
-        first_end(0)
-        crossing(3)
-        crossed(3)
-        second_end(0)
-        second_end(1)
-        inv = keep.tile([P, TILES * S], F32, name="inv", tag="prod_then_inv", align_bytes=64)
-        invert(0)
-        first_end(1)
-        difference(0)
-        difference(1)
-        invert(1)
-        second_end(2)
-        second_end(3)
-        weight(0)
-        shift(0)
-        square(2)
-        invert(2)
-        first_end(2)
-        presum(2)
-        presum(3)
-        weight(1)
-        hidden(0)
-        shift(1)
-        first_end(3)
-        difference(2)
-        square(3)
-        invert(3)
-        difference(3)
-        hidden(1)
-        weight(2)
-        weight(3)
-        shift(2)
-        hidden(2)
-        shift(3,2)
-        turn_back(0, 0, nc.scalar.copy)
-        turn_back(1, 1, nc.scalar.copy)
-        hidden(3,2)
-        turn_back(2, 2, nc.scalar.copy)
-        turn_back(3, 6, nc.scalar.copy)
-        shade(0, (4, 5), (nc.scalar.copy, nc.scalar.copy))
-        shade(1, (0, 1), (nc.vector.tensor_copy, nc.scalar.copy))
+        for t in range(TILES):
+            fetch_signs(t)
+            sum_magnitudes(t)
+            if t == 0:
+                for early in quarter_tiles(0):
+                    scale_features(early)
+            if t >= 2:
+                square_den(t - 2)
+            if t >= 1:
+                crossing(t - 1)
+                if t - 1 in quarter_tiles(0):
+                    weigh_crossing(t - 1)
+            if t < EARLY_FA_QUARTERS:
+                fetch_neg_fa(t)
+            if t == 1:
+                for u in quarter_tiles(t):
+                    turn_abs2(u)
+        crossing(TILES - 1)
+        for t in quarter_tiles(2):
+            scale_features(t)
+        for u in quarter_tiles(2):
+            turn_abs2(u)
+        fetch_fb(0)
+
+        inv = keep.tile([P, QUARTERS * S], F32, name="inv", tag="prod_then_inv", align_bytes=64)
+        last = QUARTERS - 1
+        for u in range(QUARTERS):
+            nc.scalar.activation(out=inv[:, cols(u, S)], in_=den_sq[u][:], func=ACT.Abs_reciprocal_sqrt)
+            if u < last:
+                fetch_fb(u + 1)
+                if u + 1 >= 2:
+                    square_den(u + 1)
+                if u + 1 >= EARLY_FA_QUARTERS:
+                    fetch_neg_fa(u + 1)
+            sum_fixed(u)
+            if u == 1:
+                for t in quarter_tiles(2):
+                    weigh_crossing(t)
+            weigh(u)
+            if u >= 1:
+                make_hidden(u - 1)
+            if u < last:
+                make_pull(u, whole)
+        for j in range(2):
+            make_pull(last, cols(j, HALF))
+
+        hid = [sb("hid%d" % i, len(piece) * PACK * P, BF16) for i, piece in enumerate(PIECES)]
+
+        def turn_back(i):
+            for place, b in enumerate(PIECES[i]):
+                back = bank(b, "back%d" % b)
+                words = hid_turned[:, cols(b, H)].bitcast(F32)
+                for w in range(2):
+                    nc.tensor.transpose(back[:, cols(w, P)], words[:, w : 2 * P : 2], ident[:])
+                nc.scalar.copy(
+                    out=hid[i][:, cols(place, PACK * P)].bitcast(F32).rearrange("p (e w) -> p e w", w=2),
+                    in_=back[:, 0 : 2 * P].rearrange("p (w e) -> p e w", w=2),
+                )
+
+        def shade(i):
+            width = len(PIECES[i]) * P
+            codes = sb("codes%d" % i, width, U32)
+            code_scales = sb("code_scales%d" % i, width, U8)
+            nc.vector.quantize_mx(out=codes[:].bitcast(FP8X4), scales=code_scales[:], in_=hid[i][:])
+            for m in range(OUT_TILES):
+                acc = bank((QUARTERS + OUT_TILES * i + m) % BANKS, "shade%d_%d" % (i, m))
+                nc.tensor.matmul_mx(
+                    out=acc[:, 0:width],
+                    lhsT=w3w[:, cols(m, 2 * P)].bitcast(FP4X4),
+                    lhsT_scale=w3s[:, cols(m, P)],
+                    rhs=codes[:].bitcast(FP8X4),
+                    rhs_scale=code_scales[:],
+                    start=True,
+                    stop=True,
+                )
+                copy = nc.vector.tensor_copy if i >= 1 and m == 0 else nc.scalar.copy
+                copy(out=shaded[m][:, PIECES[i][0] * P : PIECES[i][0] * P + width], in_=acc[:, 0:width])
+
+        turn_back(0)
+        for j in range(2):
+            make_hidden_block(last, j)
+        for i in range(1, len(PIECES)):
+            turn_back(i)
+        for i in range(len(PIECES)):
+            shade(i)
 
         for h in range(2):
             c = cols(h, HALF)

from contextlib import ExitStack

import concourse.mybir as mybir
from concourse.masks import make_identity

K, T, S, N, H = 512, 2048, 512, 256, 512
FLOPS = 2 * K * H * S * 2 + 2 * H * N * S

F32 = mybir.dt.float32
BF16 = mybir.dt.bfloat16
I32 = mybir.dt.int32
U32 = mybir.dt.uint32
U16 = mybir.dt.uint16
U8 = mybir.dt.uint8
FP8X4 = mybir.dt.float8_e4m3fn_x4
FP4X4 = mybir.dt.float4_e2m1fn_x4
ACT = mybir.ActivationFunctionType
ALU = mybir.AluOpType

P = 128
PACK = 4
TILES = H // P
BLOCKS = S // P
QUARTERS = 4
OUT_TILES = N // P
HALF = S // 2
LIST_COLS = S // 16
BANKS = 8
SCALAR_FT_TILES = 2
EARLY_FA_QUARTERS = 1
PIECES = ((0, 1), (2,), (3,))


def tile_picked_ymarch_off_p_kernel(
    tc, x_words, x_scales, w1_words, w1_scales, w2_words, w2_scales, unit, w3_words, w3_scales, offs, e1, e2, fc, out
):
    nc = tc.nc
    with ExitStack() as ctx:
        keep = ctx.enter_context(tc.tile_pool(name="keep", bufs=1))
        psum = ctx.enter_context(tc.psum_pool(name="psum", bufs=1))

        def sb(name, width, dtype=F32):
            return keep.tile([P, width], dtype, name=name, align_bytes=64)

        def four(name):
            return [sb("%s%d" % (name, i), S) for i in range(4)]

        def bank(slot, name):
            return psum.tile([P, S], F32, name=name, tag="bank%d" % slot)

        def cols(i, width):
            return slice(i * width, (i + 1) * width)

        def half_of(lst, h):
            return lst[:, cols(h, LIST_COLS // 2)]

        def load_scales(plane, src):
            for q in range(4):
                nc.sync.dma_start(out=plane[32 * q : 32 * q + 4, :].bitcast(I32), in_=src[0, 4 * q : 4 * q + 4, :].bitcast(I32))

        offs_sb = keep.tile([P, LIST_COLS], U16, name="offs_sb")
        e1_sb = keep.tile([P, LIST_COLS], U16, name="e1_sb")
        e2_sb = keep.tile([P, LIST_COLS], U16, name="e2_sb")
        fc_sb = keep.tile([P, LIST_COLS], U16, name="fc_sb")
        xw = sb("xw", T, U32)
        xs = sb("xs", T, U8)
        w1w = sb("w1w", 2 * H, U8)
        w2w = sb("w2w", 2 * H, U8)
        w3w = sb("w3w", 2 * N, U8)
        w1s = sb("w1s", H, U8)
        w2s = sb("w2s", H, U8)
        w3s = sb("w3s", N, U8)
        unit_sb = sb("unit_sb", TILES)
        ident = sb("ident", P)

        for plane in (xs, w2s, w1s, w3s):
            nc.vector.memset(plane[:].bitcast(I32), 0)
        nc.gpsimd.dma_start(out=w2w[:].bitcast(I32), in_=w2_words[0].bitcast(I32))
        nc.sync.dma_start(out=offs_sb[:], in_=offs)
        nc.sync.dma_start(out=xw[:].bitcast(I32), in_=x_words[0].rearrange("p n t -> p (n t)").bitcast(I32))
        load_scales(xs, x_scales)
        load_scales(w2s, w2_scales)
        nc.gpsimd.dma_start(out=w1w[:].bitcast(I32), in_=w1_words[0].bitcast(I32))
        load_scales(w1s, w1_scales)
        nc.sync.dma_start(out=e1_sb[:], in_=e1)
        nc.sync.dma_start(out=e2_sb[:], in_=e2)
        nc.sync.dma_start(out=fc_sb[:], in_=fc)
        with nc.allow_non_contiguous_dma(reason="one value of unit for each partition and tile"):
            nc.gpsimd.dma_start(out=unit_sb[:].rearrange("p (t o) -> p t o", o=1), in_=unit.rearrange("(t p) o -> p t o", p=P))
        make_identity(nc, ident[:])
        nc.gpsimd.dma_start(out=w3w[:].bitcast(I32), in_=w3_words[0].bitcast(I32))
        load_scales(w3s, w3_scales)

        xg = sb("xg", S, U32)
        xgs = sb("xgs", S, U8)
        nc.vector.tensor_copy(out=xg[:], in_=xw[:].indirect(offs_sb[:]))
        for h in range(2):
            nc.vector.tensor_copy(out=xgs[:, cols(h, HALF)], in_=xs[:].indirect(half_of(offs_sb, h)))

        def corner_product(acc, words, scales, t, c):
            nc.tensor.matmul_mx(
                out=acc[:, c],
                lhsT=words[:, cols(t, 2 * P)].bitcast(FP4X4),
                lhsT_scale=scales[:, cols(t, P)],
                rhs=xg[:, c].bitcast(FP8X4),
                rhs_scale=xgs[:, c],
                start=True,
                stop=True,
            )

        th, ft, s1, s2, abs1, abs2 = (four(n) for n in ("th", "ft", "s1_", "s2_", "abs1_", "abs2_"))
        cross, neg_us1, neg_cs, fb, neg_fa, fixed = (four(n) for n in ("cross", "neg_us1_", "neg_cs", "fb", "neg_fa", "fixed"))
        den_sq, weight, pull = (four(n) for n in ("den_sq", "weight", "pull"))
        prod = keep.tile([P, TILES * S], F32, name="prod", tag="prod_then_inv", align_bytes=64)
        hid_turned = sb("hid_turned", BLOCKS * H, BF16)
        shaded = [sb("shaded%d" % m, S) for m in range(OUT_TILES)]
        result = [sb("result%d" % m, S) for m in range(OUT_TILES)]
        ft_acc, den, abs2_turned, diff, fixed_turned = {}, {}, {}, {}, {}

        whole = slice(0, S)
        sd_acc = bank(0, "sd_acc0")
        first_sigmoid = sb("first_sigmoid", HALF)
        corner_product(sd_acc, w2w, w2s, 0, cols(0, HALF))
        nc.scalar.activation(out=first_sigmoid[:], in_=sd_acc[:, cols(0, HALF)], func=ACT.Sigmoid, scale=2.0)
        nc.scalar.activation(out=th[0][:, cols(0, HALF)], in_=first_sigmoid[:], func=ACT.Identity, scale=2.0, bias=-1.0)
        corner_product(sd_acc, w2w, w2s, 0, cols(1, HALF))
        nc.scalar.activation(out=th[0][:, cols(1, HALF)], in_=sd_acc[:, cols(1, HALF)], func=ACT.Tanh)
        for t in range(1, TILES):
            sd_acc = bank(t, "sd_acc%d" % t)
            corner_product(sd_acc, w2w, w2s, t, whole)
            nc.scalar.activation(out=th[t][:], in_=sd_acc[:], func=ACT.Tanh)
        for t in range(TILES):
            ft_acc[t] = bank(TILES + t, "ft_acc%d" % t)
            corner_product(ft_acc[t], w1w, w1s, t, whole)

        def quarter_tiles(u):
            return (u // 2 * 2, u // 2 * 2 + 1)

        def cells(u):
            return [(t, u % 2 * 2 + j, cols(2 * j + t % 2, P)) for t in quarter_tiles(u) for j in range(2)]

        def turn(acc_cols, terms, b):
            for i, term in enumerate(terms):
                nc.tensor.matmul(
                    acc_cols,
                    lhsT=term[:, cols(b, P)],
                    rhs=ident[:],
                    start=(i == 0),
                    stop=(i == len(terms) - 1),
                    is_transpose=True,
                )

        def fetch_signs(t):
            for dst, lst in ((s1[t], e1_sb), (s2[t], e2_sb)):
                for h in range(2):
                    nc.vector.tensor_copy(out=dst[:, cols(h, HALF)], in_=th[t][:].indirect(half_of(lst, h)))
            nc.gpsimd.tensor_tensor(out=prod[:, cols(t, S)], in0=s1[t][:], in1=s2[t][:], op=ALU.mult)

        def sum_magnitudes(t):
            nc.gpsimd.tensor_scalar(
                out=neg_us1[t][:], in0=s1[t][:], scalar1=unit_sb[:, t : t + 1], scalar2=-1.0, op0=ALU.mult, op1=ALU.mult
            )
            nc.scalar.activation(out=abs1[t][:], in_=s1[t][:], func=ACT.Abs)
            nc.scalar.activation(out=abs2[t][:], in_=s2[t][:], func=ACT.Abs)
            for u in quarter_tiles(t):
                if t % 2 == 0:
                    den[u] = bank(u, "den%d" % u)
                for cell_tile, b, c in cells(u):
                    if cell_tile == t:
                        turn(den[u][:, c], [abs1[t], abs2[t]], b)

        def scale_features(t):
            if t < SCALAR_FT_TILES:
                nc.scalar.activation(out=ft[t][:], in_=ft_acc[t][:], func=ACT.Copy, scale=unit_sb[:, t : t + 1])
            else:
                nc.vector.tensor_scalar(out=ft[t][:], in0=ft_acc[t][:], scalar1=unit_sb[:, t : t + 1], scalar2=None, op0=ALU.mult)

        def crossing(t):
            nc.scalar.activation(out=cross[t][:], in_=prod[:, cols(t, S)], func=ACT.Sigmoid, scale=-4.0)

        def weigh_crossing(t):
            nc.gpsimd.tensor_tensor(out=neg_cs[t][:], in0=cross[t][:], in1=neg_us1[t][:], op=ALU.mult)

        def turn_abs2(u):
            abs2_turned[u] = bank(QUARTERS + u, "abs2_turned%d" % u)
            for t, b, c in cells(u):
                turn(abs2_turned[u][:, c], [abs2[t]], b)

        def square_den(u):
            nc.scalar.activation(out=den_sq[u][:], in_=den[u][:], func=ACT.Square, bias=0.2)

        def fetch_fb(u):
            for t in quarter_tiles(u):
                nc.vector.tensor_copy(out=fb[t][:, cols(u % 2, HALF)], in_=ft[t][:].indirect(half_of(e2_sb, u % 2)))

        def fetch_neg_fa(u):
            for t in quarter_tiles(u):
                nc.scalar.activation(
                    out=neg_fa[t][:, cols(u % 2, HALF)], in_=ft[t][:].indirect(half_of(e1_sb, u % 2)), func=ACT.Copy, scale=-1.0
                )

        def sum_fixed(u):
            c = cols(u % 2, HALF)
            for t in quarter_tiles(u):
                nc.gpsimd.tensor_tensor(out=fixed[t][:, c], in0=neg_cs[t][:, c], in1=fb[t][:, c], op=ALU.add)

        def weigh(u):
            diff[u] = bank(u, "diff%d" % u)
            for t, b, c in cells(u):
                turn(diff[u][:, c], [neg_fa[t], fb[t]], b)
            nc.vector.scalar_tensor_tensor(
                out=weight[u][:], in0=abs2_turned[u][:], scalar=0.1, in1=inv[:, cols(u, S)], op0=ALU.add, op1=ALU.mult
            )
            fixed_turned[u] = bank(QUARTERS + u, "fixed_turned%d" % u)
            for t, b, c in cells(u):
                turn(fixed_turned[u][:, c], [fixed[t]], b)

        def make_pull(u, c):
            nc.vector.tensor_tensor(out=pull[u][:, c], in0=diff[u][:, c], in1=weight[u][:, c], op=ALU.mult)

        def make_hidden(u):
            nc.vector.tensor_tensor(
                out=hid_turned[:].rearrange("p (b f) -> p b f", f=H)[:, cols(u % 2, 2), cols(u // 2, 2 * P)],
                in0=fixed_turned[u][:].rearrange("p (b f) -> p b f", b=2),
                in1=pull[u][:].rearrange("p (b f) -> p b f", b=2),
                op=ALU.subtract,
            )

        def make_hidden_block(u, j):
            first = (u % 2 * 2 + j) * H + u // 2 * 2 * P
            nc.vector.tensor_tensor(
                out=hid_turned[:, first : first + 2 * P],
                in0=fixed_turned[u][:, cols(j, HALF)],
                in1=pull[u][:, cols(j, HALF)],
                op=ALU.subtract,
            )

        for t in range(TILES):
            fetch_signs(t)
            sum_magnitudes(t)
            if t == 0:
                for early in quarter_tiles(0):
                    scale_features(early)
            if t >= 2:
                square_den(t - 2)
            if t >= 1:
                crossing(t - 1)
                if t - 1 in quarter_tiles(0):
                    weigh_crossing(t - 1)
            if t < EARLY_FA_QUARTERS:
                fetch_neg_fa(t)
            if t == 1:
                for u in quarter_tiles(t):
                    turn_abs2(u)
        crossing(TILES - 1)
        for t in quarter_tiles(2):
            scale_features(t)
        for u in quarter_tiles(2):
            turn_abs2(u)
        fetch_fb(0)

        inv = keep.tile([P, QUARTERS * S], F32, name="inv", tag="prod_then_inv", align_bytes=64)
        last = QUARTERS - 1
        for u in range(QUARTERS):
            nc.scalar.activation(out=inv[:, cols(u, S)], in_=den_sq[u][:], func=ACT.Abs_reciprocal_sqrt)
            if u < last:
                fetch_fb(u + 1)
                if u + 1 >= 2:
                    square_den(u + 1)
                if u + 1 >= EARLY_FA_QUARTERS:
                    fetch_neg_fa(u + 1)
            sum_fixed(u)
            if u == 1:
                for t in quarter_tiles(2):
                    weigh_crossing(t)
            weigh(u)
            if u >= 1:
                make_hidden(u - 1)
            if u < last:
                make_pull(u, whole)
        for j in range(2):
            make_pull(last, cols(j, HALF))

        hid = [sb("hid%d" % i, len(piece) * PACK * P, BF16) for i, piece in enumerate(PIECES)]

        def turn_back(i):
            for place, b in enumerate(PIECES[i]):
                back = bank(b, "back%d" % b)
                words = hid_turned[:, cols(b, H)].bitcast(F32)
                for w in range(2):
                    nc.tensor.transpose(back[:, cols(w, P)], words[:, w : 2 * P : 2], ident[:])
                nc.scalar.copy(
                    out=hid[i][:, cols(place, PACK * P)].bitcast(F32).rearrange("p (e w) -> p e w", w=2),
                    in_=back[:, 0 : 2 * P].rearrange("p (w e) -> p e w", w=2),
                )

        def shade(i):
            width = len(PIECES[i]) * P
            codes = sb("codes%d" % i, width, U32)
            code_scales = sb("code_scales%d" % i, width, U8)
            nc.vector.quantize_mx(out=codes[:].bitcast(FP8X4), scales=code_scales[:], in_=hid[i][:])
            for m in range(OUT_TILES):
                acc = bank((QUARTERS + OUT_TILES * i + m) % BANKS, "shade%d_%d" % (i, m))
                nc.tensor.matmul_mx(
                    out=acc[:, 0:width],
                    lhsT=w3w[:, cols(m, 2 * P)].bitcast(FP4X4),
                    lhsT_scale=w3s[:, cols(m, P)],
                    rhs=codes[:].bitcast(FP8X4),
                    rhs_scale=code_scales[:],
                    start=True,
                    stop=True,
                )
                copy = nc.vector.tensor_copy if i >= 1 and m == 0 else nc.scalar.copy
                copy(out=shaded[m][:, PIECES[i][0] * P : PIECES[i][0] * P + width], in_=acc[:, 0:width])

        turn_back(0)
        for j in range(2):
            make_hidden_block(last, j)
        for i in range(1, len(PIECES)):
            turn_back(i)
        for i in range(len(PIECES)):
            shade(i)

        for h in range(2):
            c = cols(h, HALF)
            nc.vector.tensor_copy(out=result[0][:, c], in_=shaded[0][:].indirect(half_of(fc_sb, h)))
            nc.sync.dma_start(out=out[0:P, c], in_=result[0][:, c])
            nc.scalar.activation(out=result[1][:, c], in_=shaded[1][:].indirect(half_of(fc_sb, h)), func=ACT.Copy)
            nc.sync.dma_start(out=out[P : 2 * P, c], in_=result[1][:, c])
